import numpy as np
import ml_dtypes


def mxq(x, axis, fmt="e4m3"):
    dtype, down = {"e4m3": (ml_dtypes.float8_e4m3fn, 7), "e5m2": (ml_dtypes.float8_e5m2, 14)}[fmt]
    v = np.moveaxis(np.asarray(x, np.float32).astype(ml_dtypes.bfloat16).astype(np.float64), axis, -1)
    blocks = v.reshape(v.shape[:-1] + (-1, 32))
    amax = np.abs(blocks).max(-1, keepdims=True)
    byte = np.maximum(np.where(amax > 0, np.frexp(amax)[1] - 1 + 127, 0) - down, 1)
    scale = np.exp2(byte - 127.0)
    codes = (blocks / scale).astype(np.float32).astype(dtype).astype(np.float64)
    return np.moveaxis((codes * scale).reshape(v.shape), -1, axis)


WIDE = False


def mx_kscale(k):
    if not WIDE:
        return np.ones(k)
    levels = np.array([10, -10, 5, -5, 0])
    if k % 512:
        return np.exp2(np.random.permutation(np.resize(levels, k // 32))).repeat(32)
    a = np.empty((k // 512, 16))
    for p in range(k // 512):
        a[p, :8] = np.random.permutation(np.resize(levels, 8))
        for g in range(8):
            far = levels[np.abs(levels - a[p, g]) >= 10]
            a[p, g + 8] = far[np.random.randint(len(far))]
    return np.exp2(a.ravel()).repeat(32)


def f64(x):
    return np.asarray(x).astype(np.float64)


def striped(idx):
    return np.tile(idx.reshape(-1, 16).T, (8, 1)).astype(np.uint16)


def unstriped(offs):
    return offs[:16].T.reshape(-1).astype(np.int64)


def relu(v):
    return np.maximum(v, 0.0)


K, T, S, V, N = 1024, 2048, 768, 384, 128


def setup_inputs():
    n = np.random.standard_normal
    s = mx_kscale(K)[:, None]
    return {
        "xT": (n((K, T)) * s).astype(np.float32),
        "w1": (n((K, N)) / np.sqrt(K) / s).astype(np.float32),
        "w2": (n((K, N)) / np.sqrt(K) / s).astype(np.float32),
        "offs": striped(np.random.permutation(T)[:S]),
    }


def reference(xT, w1, w2, offs):
    xq = mxq(f64(xT)[:, unstriped(offs)], 0, "e4m3")
    e = np.exp(mxq(f64(w1), 0, "e4m3").T @ xq)
    h = mxq(f64(w2), 0, "e4m3").T @ xq
    num = e[:, :V] * h[:, :V] + e[:, V:2 * V] * h[:, V:2 * V]
    den = e[:, :V] + e[:, V:2 * V]
    return relu(num / den)

@@ -1,0 +1,198 @@
+from contextlib import ExitStack
+
+import concourse.mybir as mybir
+
+K, T, S, V, N = 1024, 2048, 768, 384, 128
+FLOPS = 2 * 2 * K * N * S
+
+F32 = mybir.dt.float32
+BF16 = mybir.dt.bfloat16
+U32 = mybir.dt.uint32
+U16 = mybir.dt.uint16
+U8 = mybir.dt.uint8
+FP8X4 = mybir.dt.float8_e4m3fn_x4
+ACT = mybir.ActivationFunctionType
+ALU = mybir.AluOpType
+
+P = 128
+PACK = 4
+PASSES = K // (P * PACK)
+CHUNK = 256
+CHUNKS = S // CHUNK
+LIST_COLS = CHUNK // 16
+EARLY = 2 * CHUNK - V
+
+
+def weave(dst, src):
+    return dst.rearrange("p (c i) j -> p c j i", i=4), src.rearrange("p j (c i) -> p c j i", i=4)
+
+
+def tile_picked_apool_relu_e_kernel(tc, xT, w1, w2, offs, out):
+    nc = tc.nc
+    with ExitStack() as ctx:
+        keep = ctx.enter_context(tc.tile_pool(name="keep", bufs=1))
+        psum = ctx.enter_context(tc.psum_pool(name="psum", bufs=1))
+
+        offsets = keep.tile([P, S // 16], U16, name="offsets")
+        w_raw = {(m, z): keep.tile([P, PACK, N], F32, name="w%d_raw%d" % (m, z)) for m in (1, 2) for z in range(PASSES)}
+        plane = [[keep.tile([P, T], F32, name="plane%d_%d" % (z, j)) for j in range(PACK)] for z in range(PASSES)]
+        x_rows = xT.rearrange("(z p j) t -> z j p t", z=PASSES, j=PACK)
+        w_rows = {1: w1.rearrange("(z p j) m -> z p j m", z=PASSES, j=PACK), 2: w2.rearrange("(z p j) m -> z p j m", z=PASSES, j=PACK)}
+        late = []
+        early = [key for key in w_raw if key not in late]
+        for m, z in early:
+            nc.sync.dma_start(out=w_raw[m, z][:], in_=w_rows[m][z])
+        nc.sync.dma_start(offsets[:], offs)
+        for z in range(PASSES):
+            for j in range(PACK):
+                nc.sync.dma_start(out=plane[z][j][:], in_=x_rows[z, j])
+        for m, z in late:
+            nc.sync.dma_start(out=w_raw[m, z][:], in_=w_rows[m][z])
+
+        def mx_tiles(name, width):
+            return (keep.tile([P, width], U32, name=name + "_codes", align_bytes=64),
+                    keep.tile([P, width], U8, name=name + "_scales", align_bytes=64))
+
+        def quantize(mx, cols, grouped):
+            nc.vector.quantize_mx(out=mx[0][:, cols].bitcast(FP8X4), scales=mx[1][:, cols], in_=grouped)
+
+        def product(acc, w, x_codes, cols, start, stop):
+            nc.tensor.matmul_mx(out=acc, lhsT=w[0][:].bitcast(FP8X4), lhsT_scale=w[1][:],
+                                rhs=x_codes[0][:, cols].bitcast(FP8X4), rhs_scale=x_codes[1][:, cols], start=start, stop=stop)
+
+        w_mx = {}
+        w_grouped = {}
+
+        def weave_weights(m, z, sign):
+            w_grouped[m, z, sign] = keep.tile([P, N, PACK], BF16, name="wg%d_%d_%d" % (m, z, sign + 1), align_bytes=64)
+            dst, src = weave(w_grouped[m, z, sign][:], w_raw[m, z][:])
+            nc.scalar.activation(dst, src, ACT.Copy, scale=float(sign))
+
+        def quantize_weights(m, z, sign):
+            w_mx[m, z, sign] = mx_tiles("w%d_%d_%d" % (m, z, sign + 1), N)
+            quantize(w_mx[m, z, sign], slice(0, N), w_grouped[m, z, sign][:].rearrange("p m j -> p (m j)"))
+
+        def signed(keys):
+            return [(m, z, sign) for m, z in keys for sign in ((-1, 1) if m == 1 else (1,))]
+
+        for key in signed(early):
+            weave_weights(*key)
+            quantize_weights(*key)
+
+        SLOTS = 2
+        WOVEN = []
+        upper = {c: keep.tile([P, 2, CHUNK], F32, name="upper%d" % c) for c in WOVEN}
+        x_mx = [mx_tiles("x%d" % z, S) for z in range(PASSES)]
+        picked = [[keep.tile([P, PACK if z == 0 else SLOTS, CHUNK], F32, name="picked%d_%d" % (z, c)) for c in range(CHUNKS)]
+                  for z in range(PASSES)]
+        grouped = [[keep.tile([P, CHUNK, PACK], BF16, name="grouped%d_%d" % (z, c), align_bytes=64) for c in range(CHUNKS)]
+                   for z in range(PASSES)]
+
+        def gather(dst, z, j, c):
+            nc.vector.tensor_copy(dst, plane[z][j][:].indirect(offsets[:, c * LIST_COLS:(c + 1) * LIST_COLS]))
+
+        def quantize_chunk(z, c):
+            quantize(x_mx[z], slice(c * CHUNK, (c + 1) * CHUNK), grouped[z][c][:].rearrange("p n j -> p (n j)"))
+
+        h_banks = [(cols, psum.tile([P, cols.stop - cols.start], F32, name="h%d" % cols.start)) for cols in (slice(0, 512), slice(512, 640), slice(640, 768))]
+        diff = [psum.tile([P, 128], F32, name="diff%d" % g) for g in range(3)]
+
+        def d_neg(z, g):
+            product(diff[g][:], w_mx[1, z, -1], x_mx[z], slice(128 * g, 128 * (g + 1)), z == 0, False)
+
+        def d_pos(z, g):
+            product(diff[g][:], w_mx[1, z, 1], x_mx[z], slice(V + 128 * g, V + 128 * (g + 1)), False, z == 1)
+
+        def h_mm(z, b):
+            product(h_banks[b][1][:], w_mx[2, z, 1], x_mx[z], h_banks[b][0], z == 0, z == 1)
+
+        def h_at(first):
+            for cols, bank in h_banks:
+                if cols.start <= first < cols.stop:
+                    return bank[:, first - cols.start:first - cols.start + 128]
+
+        def last_plane(c):
+            if c in WOVEN:
+                gather(upper[c][:, 1, :], 1, 3, c)
+                dst, src = weave(grouped[1][c][:, :, 2:4], upper[c][:])
+                nc.scalar.copy(dst, src)
+            else:
+                gather(grouped[1][c][:, :, 3], 1, 3, c)
+
+        def quantize_half(c, half):
+            first = c * CHUNK + half * 128
+            quantize(x_mx[1], slice(first, first + 128), grouped[1][c][:, half * 128:(half + 1) * 128, :].rearrange("p n j -> p (n j)"))
+
+        tiles = [[keep.tile([P, 128], F32, name="%s%d" % (n, g)) for n in ("tanh", "u", "t", "o", "result")] for g in range(3)]
+
+        def stage_a(g):
+            nc.scalar.activation(tiles[g][0][:], diff[g][:], ACT.Tanh, scale=0.5)
+
+        def stage_u(g):
+            nc.vector.scalar_tensor_tensor(tiles[g][1][:], tiles[g][0][:], 1.0, h_at(128 * g), ALU.subtract, ALU.mult)
+
+        def stage_t(g):
+            nc.vector.scalar_tensor_tensor(tiles[g][2][:], tiles[g][0][:], 1.0, h_at(V + 128 * g), ALU.add, ALU.mult)
+
+        def stage_o(g):
+            nc.vector.tensor_tensor(tiles[g][3][:], tiles[g][2][:], tiles[g][1][:], ALU.subtract)
+            nc.scalar.activation(tiles[g][4][:], tiles[g][3][:], ACT.Relu, scale=0.5)
+            nc.sync.dma_start(out=out[:, 128 * g:128 * (g + 1)], in_=tiles[g][4][:])
+
+        for j in range(PACK):
+            for c in range(CHUNKS):
+                gather(picked[0][c][:, j, :], 0, j, c)
+        for c in range(CHUNKS):
+            dst, src = weave(grouped[0][c][:], picked[0][c][:])
+            nc.scalar.copy(dst, src)
+        for j in range(SLOTS):
+            for c in range(CHUNKS):
+                gather(picked[1][c][:, j, :], 1, j, c)
+            if j < 2:
+                for c in ((0,), (1, 2))[j]:
+                    quantize_chunk(0, c)
+        for c in range(CHUNKS):
+            dst, src = weave(grouped[1][c][:, :, 0:SLOTS], picked[1][c][:])
+            nc.scalar.copy(dst, src)
+        for j in range(SLOTS, PACK - 1):
+            for c in range(CHUNKS):
+                gather(upper[c][:, 0, :] if c in WOVEN else grouped[1][c][:, :, j], 1, j, c)
+        for key in signed(late):
+            weave_weights(*key)
+        if (1, 0) in early:
+            for g in range(3):
+                d_neg(0, g)
+            for g in range(3):
+                d_pos(0, g)
+        if (2, 0) in early:
+            for b in range(len(h_banks)):
+                h_mm(0, b)
+
+        last_plane(0)
+        last_plane(1)
+        quantize_chunk(1, 0)
+        quantize_chunk(1, 1)
+        last_plane(2)
+        d_neg(1, 0)
+        d_pos(1, 0)
+        h_mm(1, 0)
+        d_neg(1, 1)
+        d_neg(1, 2)
+        quantize_half(2, 0)
+        quantize_half(2, 1)
+        d_pos(1, 1)
+        d_pos(1, 2)
+        h_mm(1, 1)
+        h_mm(1, 2)
+        stage_a(0)
+        stage_u(0)
+        stage_t(0)
+        stage_o(0)
+        stage_a(1)
+        stage_a(2)
+        stage_u(1)
+        stage_t(1)
+        stage_u(2)
+        stage_t(2)
+        stage_o(1)
+        stage_o(2)

@@ -38,16 +38,19 @@ def tile_picked_apool_relu_e_kernel(tc, xT, w1, w2, offs, out):
         plane = [[keep.tile([P, T], F32, name="plane%d_%d" % (z, j)) for j in range(PACK)] for z in range(PASSES)]
         x_rows = xT.rearrange("(z p j) t -> z j p t", z=PASSES, j=PACK)
         w_rows = {1: w1.rearrange("(z p j) m -> z p j m", z=PASSES, j=PACK), 2: w2.rearrange("(z p j) m -> z p j m", z=PASSES, j=PACK)}
-        late = []
-        early = [key for key in w_raw if key not in late]
-        for m, z in early:
-            nc.sync.dma_start(out=w_raw[m, z][:], in_=w_rows[m][z])
+        nc.sync.dma_start(out=plane[0][0][:], in_=x_rows[0, 0])
         nc.sync.dma_start(offsets[:], offs)
-        for z in range(PASSES):
-            for j in range(PACK):
-                nc.sync.dma_start(out=plane[z][j][:], in_=x_rows[z, j])
-        for m, z in late:
-            nc.sync.dma_start(out=w_raw[m, z][:], in_=w_rows[m][z])
+        nc.sync.dma_start(out=plane[0][1][:], in_=x_rows[0, 1])
+        nc.sync.dma_start(out=plane[0][2][:], in_=x_rows[0, 2])
+        nc.sync.dma_start(out=plane[0][3][:], in_=x_rows[0, 3])
+        nc.sync.dma_start(out=w_raw[1, 1][:], in_=w_rows[1][1])
+        nc.sync.dma_start(out=plane[1][0][:], in_=x_rows[1, 0])
+        nc.sync.dma_start(out=plane[1][1][:], in_=x_rows[1, 1])
+        nc.sync.dma_start(out=plane[1][2][:], in_=x_rows[1, 2])
+        nc.sync.dma_start(out=w_raw[1, 0][:], in_=w_rows[1][0])
+        nc.sync.dma_start(out=w_raw[2, 0][:], in_=w_rows[2][0])
+        nc.sync.dma_start(out=plane[1][3][:], in_=x_rows[1, 3])
+        nc.sync.dma_start(out=w_raw[2, 1][:], in_=w_rows[2][1])
 
         def mx_tiles(name, width):
             return (keep.tile([P, width], U32, name=name + "_codes", align_bytes=64),
@@ -75,26 +78,28 @@ def tile_picked_apool_relu_e_kernel(tc, xT, w1, w2, offs, out):
         def signed(keys):
             return [(m, z, sign) for m, z in keys for sign in ((-1, 1) if m == 1 else (1,))]
 
-        for key in signed(early):
-            weave_weights(*key)
-            quantize_weights(*key)
+        def weights(m, z):
+            for key in signed([(m, z)]):
+                weave_weights(*key)
+                quantize_weights(*key)
 
-        SLOTS = 2
-        WOVEN = []
-        upper = {c: keep.tile([P, 2, CHUNK], F32, name="upper%d" % c) for c in WOVEN}
         x_mx = [mx_tiles("x%d" % z, S) for z in range(PASSES)]
-        picked = [[keep.tile([P, PACK if z == 0 else SLOTS, CHUNK], F32, name="picked%d_%d" % (z, c)) for c in range(CHUNKS)]
-                  for z in range(PASSES)]
-        grouped = [[keep.tile([P, CHUNK, PACK], BF16, name="grouped%d_%d" % (z, c), align_bytes=64) for c in range(CHUNKS)]
-                   for z in range(PASSES)]
+        picked = [[keep.tile([P, (PACK, 2)[z], CHUNK], F32, name="picked%d_%d" % (z, c)) for c in range(CHUNKS)] for z in range(PASSES)]
+        grouped = [[keep.tile([P, CHUNK, PACK], BF16, name="grouped%d_%d" % (z, c), align_bytes=64) for c in range(CHUNKS)] for z in range(PASSES)]
 
-        def gather(dst, z, j, c):
+        def gather(z, j, c, stepped):
+            dst = grouped[z][c][:, :, j] if stepped else picked[z][c][:, j, :]
             nc.vector.tensor_copy(dst, plane[z][j][:].indirect(offsets[:, c * LIST_COLS:(c + 1) * LIST_COLS]))
 
-        def quantize_chunk(z, c):
-            quantize(x_mx[z], slice(c * CHUNK, (c + 1) * CHUNK), grouped[z][c][:].rearrange("p n j -> p (n j)"))
+        def weave_x(z, c):
+            dst, src = weave(grouped[z][c][:, :, 0:(PACK, 2)[z]], picked[z][c][:])
+            nc.scalar.activation(dst, src, ACT.Copy)
 
-        h_banks = [(cols, psum.tile([P, cols.stop - cols.start], F32, name="h%d" % cols.start)) for cols in (slice(0, 512), slice(512, 640), slice(640, 768))]
+        def quantize_x(z, first, n):
+            c, at = divmod(first, CHUNK)
+            quantize(x_mx[z], slice(first, first + n), grouped[z][c][:, at:at + n, :].rearrange("p n j -> p (n j)"))
+
+        h_banks = [(cols, psum.tile([P, cols.stop - cols.start], F32, name="h%d" % cols.start)) for cols in (slice(0, 256), slice(256, 512), slice(512, 640), slice(640, 768))]
         diff = [psum.tile([P, 128], F32, name="diff%d" % g) for g in range(3)]
 
         def d_neg(z, g):
@@ -110,18 +115,6 @@ def tile_picked_apool_relu_e_kernel(tc, xT, w1, w2, offs, out):
             for cols, bank in h_banks:
                 if cols.start <= first < cols.stop:
                     return bank[:, first - cols.start:first - cols.start + 128]
-
-        def last_plane(c):
-            if c in WOVEN:
-                gather(upper[c][:, 1, :], 1, 3, c)
-                dst, src = weave(grouped[1][c][:, :, 2:4], upper[c][:])
-                nc.scalar.copy(dst, src)
-            else:
-                gather(grouped[1][c][:, :, 3], 1, 3, c)
-
-        def quantize_half(c, half):
-            first = c * CHUNK + half * 128
-            quantize(x_mx[1], slice(first, first + 128), grouped[1][c][:, half * 128:(half + 1) * 128, :].rearrange("p n j -> p (n j)"))
 
         tiles = [[keep.tile([P, 128], F32, name="%s%d" % (n, g)) for n in ("tanh", "u", "t", "o", "result")] for g in range(3)]
 
@@ -139,51 +132,53 @@ def tile_picked_apool_relu_e_kernel(tc, xT, w1, w2, offs, out):
             nc.scalar.activation(tiles[g][4][:], tiles[g][3][:], ACT.Relu, scale=0.5)
             nc.sync.dma_start(out=out[:, 128 * g:128 * (g + 1)], in_=tiles[g][4][:])
 
-        for j in range(PACK):
-            for c in range(CHUNKS):
-                gather(picked[0][c][:, j, :], 0, j, c)
-        for c in range(CHUNKS):
-            dst, src = weave(grouped[0][c][:], picked[0][c][:])
-            nc.scalar.copy(dst, src)
-        for j in range(SLOTS):
-            for c in range(CHUNKS):
-                gather(picked[1][c][:, j, :], 1, j, c)
-            if j < 2:
-                for c in ((0,), (1, 2))[j]:
-                    quantize_chunk(0, c)
-        for c in range(CHUNKS):
-            dst, src = weave(grouped[1][c][:, :, 0:SLOTS], picked[1][c][:])
-            nc.scalar.copy(dst, src)
-        for j in range(SLOTS, PACK - 1):
-            for c in range(CHUNKS):
-                gather(upper[c][:, 0, :] if c in WOVEN else grouped[1][c][:, :, j], 1, j, c)
-        for key in signed(late):
-            weave_weights(*key)
-        if (1, 0) in early:
-            for g in range(3):
-                d_neg(0, g)
-            for g in range(3):
-                d_pos(0, g)
-        if (2, 0) in early:
-            for b in range(len(h_banks)):
-                h_mm(0, b)
-
-        last_plane(0)
-        last_plane(1)
-        quantize_chunk(1, 0)
-        quantize_chunk(1, 1)
-        last_plane(2)
+        for j in range(3):
+            for c in range(3):
+                gather(0, j, c, False)
+        for c in range(3):
+            gather(0, 3, c, False)
+            weave_x(0, c)
+        for c in range(3):
+            gather(1, 0, c, False)
+        quantize_x(0, 0, 256)
+        quantize_x(0, 256, 256)
+        quantize_x(0, 512, 256)
+        weights(1, 1)
+        for c in range(3):
+            gather(1, 1, c, False)
+            weave_x(1, c)
+        for c in range(3):
+            gather(1, 2, c, True)
+        weights(1, 0)
+        weights(2, 0)
+        for g in range(3):
+            d_neg(0, g)
+        for g in range(3):
+            d_pos(0, g)
+        for b in range(len(h_banks)):
+            h_mm(0, b)
+        spare = psum.tile([P, 256], F32, name="spare")
+        for c in range(3):
+            product(spare[:], w_mx[2, 0, 1], x_mx[0], slice(256 * c, 256 * (c + 1)), True, True)
+        weave_weights(2, 1, 1)
+        for c in range(3):
+            gather(1, 3, c, True)
+        quantize_x(1, 0, 128)
+        quantize_x(1, 128, 128)
+        quantize_weights(2, 1, 1)
+        quantize_x(1, 256, 256)
+        quantize_x(1, 512, 128)
+        quantize_x(1, 640, 128)
         d_neg(1, 0)
-        d_pos(1, 0)
-        h_mm(1, 0)
         d_neg(1, 1)
+        d_pos(1, 0)
         d_neg(1, 2)
-        quantize_half(2, 0)
-        quantize_half(2, 1)
+        h_mm(1, 0)
+        h_mm(1, 1)
         d_pos(1, 1)
         d_pos(1, 2)
-        h_mm(1, 1)
         h_mm(1, 2)
+        h_mm(1, 3)
         stage_a(0)
         stage_u(0)
         stage_t(0)

@@ -87,8 +87,17 @@ def tile_picked_apool_relu_e_kernel(tc, xT, w1, w2, offs, out):
         picked = [[keep.tile([P, (PACK, 2)[z], CHUNK], F32, name="picked%d_%d" % (z, c)) for c in range(CHUNKS)] for z in range(PASSES)]
         grouped = [[keep.tile([P, CHUNK, PACK], BF16, name="grouped%d_%d" % (z, c), align_bytes=64) for c in range(CHUNKS)] for z in range(PASSES)]
 
+        upper = {c: keep.tile([P, 2, CHUNK], F32, name="upper%d" % c) for c in [0]}
+
+        def weave_upper(c):
+            dst, src = weave(grouped[1][c][:, :, 2:4], upper[c][:])
+            nc.scalar.activation(dst, src, ACT.Copy)
+
         def gather(z, j, c, stepped):
-            dst = grouped[z][c][:, :, j] if stepped else picked[z][c][:, j, :]
+            if stepped:
+                dst = upper[c][:, j - 2, :] if c in upper else grouped[z][c][:, :, j]
+            else:
+                dst = picked[z][c][:, j, :]
             nc.vector.tensor_copy(dst, plane[z][j][:].indirect(offsets[:, c * LIST_COLS:(c + 1) * LIST_COLS]))
 
         def weave_x(z, c):
@@ -160,9 +169,11 @@ def tile_picked_apool_relu_e_kernel(tc, xT, w1, w2, offs, out):
         spare = psum.tile([P, 256], F32, name="spare")
         for c in range(3):
             product(spare[:], w_mx[2, 0, 1], x_mx[0], slice(256 * c, 256 * (c + 1)), True, True)
-        weave_weights(2, 1, 1)
         for c in range(3):
             gather(1, 3, c, True)
+            if c in upper:
+                weave_upper(c)
+        weave_weights(2, 1, 1)
         quantize_x(1, 0, 128)
         quantize_x(1, 128, 128)
         quantize_weights(2, 1, 1)

from contextlib import ExitStack

import concourse.mybir as mybir

K, T, S, V, N = 1024, 2048, 768, 384, 128
FLOPS = 2 * 2 * K * N * S

F32 = mybir.dt.float32
BF16 = mybir.dt.bfloat16
U32 = mybir.dt.uint32
U16 = mybir.dt.uint16
U8 = mybir.dt.uint8
FP8X4 = mybir.dt.float8_e4m3fn_x4
ACT = mybir.ActivationFunctionType
ALU = mybir.AluOpType

P = 128
PACK = 4
PASSES = K // (P * PACK)
CHUNK = 256
CHUNKS = S // CHUNK
LIST_COLS = CHUNK // 16
EARLY = 2 * CHUNK - V


def weave(dst, src):
    return dst.rearrange("p (c i) j -> p c j i", i=4), src.rearrange("p j (c i) -> p c j i", i=4)


def tile_picked_apool_relu_e_kernel(tc, xT, w1, w2, offs, out):
    nc = tc.nc
    with ExitStack() as ctx:
        keep = ctx.enter_context(tc.tile_pool(name="keep", bufs=1))
        psum = ctx.enter_context(tc.psum_pool(name="psum", bufs=1))

        offsets = keep.tile([P, S // 16], U16, name="offsets")
        w_raw = {(m, z): keep.tile([P, PACK, N], F32, name="w%d_raw%d" % (m, z)) for m in (1, 2) for z in range(PASSES)}
        plane = [[keep.tile([P, T], F32, name="plane%d_%d" % (z, j)) for j in range(PACK)] for z in range(PASSES)]
        x_rows = xT.rearrange("(z p j) t -> z j p t", z=PASSES, j=PACK)
        w_rows = {1: w1.rearrange("(z p j) m -> z p j m", z=PASSES, j=PACK), 2: w2.rearrange("(z p j) m -> z p j m", z=PASSES, j=PACK)}
        nc.sync.dma_start(out=plane[0][0][:], in_=x_rows[0, 0])
        nc.sync.dma_start(offsets[:], offs)
        nc.sync.dma_start(out=plane[0][1][:], in_=x_rows[0, 1])
        nc.sync.dma_start(out=plane[0][2][:], in_=x_rows[0, 2])
        nc.sync.dma_start(out=plane[0][3][:], in_=x_rows[0, 3])
        nc.sync.dma_start(out=w_raw[1, 1][:], in_=w_rows[1][1])
        nc.sync.dma_start(out=plane[1][0][:], in_=x_rows[1, 0])
        nc.sync.dma_start(out=plane[1][1][:], in_=x_rows[1, 1])
        nc.sync.dma_start(out=plane[1][2][:], in_=x_rows[1, 2])
        nc.sync.dma_start(out=w_raw[1, 0][:], in_=w_rows[1][0])
        nc.sync.dma_start(out=w_raw[2, 0][:], in_=w_rows[2][0])
        nc.sync.dma_start(out=plane[1][3][:], in_=x_rows[1, 3])
        nc.sync.dma_start(out=w_raw[2, 1][:], in_=w_rows[2][1])

        def mx_tiles(name, width):
            return (keep.tile([P, width], U32, name=name + "_codes", align_bytes=64),
                    keep.tile([P, width], U8, name=name + "_scales", align_bytes=64))

        def quantize(mx, cols, grouped):
            nc.vector.quantize_mx(out=mx[0][:, cols].bitcast(FP8X4), scales=mx[1][:, cols], in_=grouped)

        def product(acc, w, x_codes, cols, start, stop):
            nc.tensor.matmul_mx(out=acc, lhsT=w[0][:].bitcast(FP8X4), lhsT_scale=w[1][:],
                                rhs=x_codes[0][:, cols].bitcast(FP8X4), rhs_scale=x_codes[1][:, cols], start=start, stop=stop)

        w_mx = {}
        w_grouped = {}

        def weave_weights(m, z, sign):
            w_grouped[m, z, sign] = keep.tile([P, N, PACK], BF16, name="wg%d_%d_%d" % (m, z, sign + 1), align_bytes=64)
            dst, src = weave(w_grouped[m, z, sign][:], w_raw[m, z][:])
            nc.scalar.activation(dst, src, ACT.Copy, scale=float(sign))

        def quantize_weights(m, z, sign):
            w_mx[m, z, sign] = mx_tiles("w%d_%d_%d" % (m, z, sign + 1), N)
            quantize(w_mx[m, z, sign], slice(0, N), w_grouped[m, z, sign][:].rearrange("p m j -> p (m j)"))

        def signed(keys):
            return [(m, z, sign) for m, z in keys for sign in ((-1, 1) if m == 1 else (1,))]

        def weights(m, z):
            for key in signed([(m, z)]):
                weave_weights(*key)
                quantize_weights(*key)

        x_mx = [mx_tiles("x%d" % z, S) for z in range(PASSES)]
        picked = [[keep.tile([P, (PACK, 2)[z], CHUNK], F32, name="picked%d_%d" % (z, c)) for c in range(CHUNKS)] for z in range(PASSES)]
        grouped = [[keep.tile([P, CHUNK, PACK], BF16, name="grouped%d_%d" % (z, c), align_bytes=64) for c in range(CHUNKS)] for z in range(PASSES)]

        upper = {c: keep.tile([P, 2, CHUNK], F32, name="upper%d" % c) for c in [0]}

        def weave_upper(c):
            dst, src = weave(grouped[1][c][:, :, 2:4], upper[c][:])
            nc.scalar.activation(dst, src, ACT.Copy)

        def gather(z, j, c, stepped):
            if stepped:
                dst = upper[c][:, j - 2, :] if c in upper else grouped[z][c][:, :, j]
            else:
                dst = picked[z][c][:, j, :]
            nc.vector.tensor_copy(dst, plane[z][j][:].indirect(offsets[:, c * LIST_COLS:(c + 1) * LIST_COLS]))

        def weave_x(z, c):
            dst, src = weave(grouped[z][c][:, :, 0:(PACK, 2)[z]], picked[z][c][:])
            nc.scalar.activation(dst, src, ACT.Copy)

        def quantize_x(z, first, n):
            c, at = divmod(first, CHUNK)
            quantize(x_mx[z], slice(first, first + n), grouped[z][c][:, at:at + n, :].rearrange("p n j -> p (n j)"))

        h_banks = [(cols, psum.tile([P, cols.stop - cols.start], F32, name="h%d" % cols.start)) for cols in (slice(0, 256), slice(256, 512), slice(512, 640), slice(640, 768))]
        diff = [psum.tile([P, 128], F32, name="diff%d" % g) for g in range(3)]

        def d_neg(z, g):
            product(diff[g][:], w_mx[1, z, -1], x_mx[z], slice(128 * g, 128 * (g + 1)), z == 0, False)

        def d_pos(z, g):
            product(diff[g][:], w_mx[1, z, 1], x_mx[z], slice(V + 128 * g, V + 128 * (g + 1)), False, z == 1)

        def h_mm(z, b):
            product(h_banks[b][1][:], w_mx[2, z, 1], x_mx[z], h_banks[b][0], z == 0, z == 1)

        def h_at(first):
            for cols, bank in h_banks:
                if cols.start <= first < cols.stop:
                    return bank[:, first - cols.start:first - cols.start + 128]

        tiles = [[keep.tile([P, 128], F32, name="%s%d" % (n, g)) for n in ("tanh", "u", "t", "o", "result")] for g in range(3)]

        def stage_a(g):
            nc.scalar.activation(tiles[g][0][:], diff[g][:], ACT.Tanh, scale=0.5)

        def stage_u(g):
            nc.vector.scalar_tensor_tensor(tiles[g][1][:], tiles[g][0][:], 1.0, h_at(128 * g), ALU.subtract, ALU.mult)

        def stage_t(g):
            nc.vector.scalar_tensor_tensor(tiles[g][2][:], tiles[g][0][:], 1.0, h_at(V + 128 * g), ALU.add, ALU.mult)

        def stage_o(g):
            nc.vector.tensor_tensor(tiles[g][3][:], tiles[g][2][:], tiles[g][1][:], ALU.subtract)
            nc.scalar.activation(tiles[g][4][:], tiles[g][3][:], ACT.Relu, scale=0.5)
            nc.sync.dma_start(out=out[:, 128 * g:128 * (g + 1)], in_=tiles[g][4][:])

        for j in range(3):
            for c in range(3):
                gather(0, j, c, False)
        for c in range(3):
            gather(0, 3, c, False)
            weave_x(0, c)
        for c in range(3):
            gather(1, 0, c, False)
        quantize_x(0, 0, 256)
        quantize_x(0, 256, 256)
        quantize_x(0, 512, 256)
        weights(1, 1)
        for c in range(3):
            gather(1, 1, c, False)
            weave_x(1, c)
        for c in range(3):
            gather(1, 2, c, True)
        weights(1, 0)
        weights(2, 0)
        for g in range(3):
            d_neg(0, g)
        for g in range(3):
            d_pos(0, g)
        for b in range(len(h_banks)):
            h_mm(0, b)
        spare = psum.tile([P, 256], F32, name="spare")
        for c in range(3):
            product(spare[:], w_mx[2, 0, 1], x_mx[0], slice(256 * c, 256 * (c + 1)), True, True)
        for c in range(3):
            gather(1, 3, c, True)
            if c in upper:
                weave_upper(c)
        weave_weights(2, 1, 1)
        quantize_x(1, 0, 128)
        quantize_x(1, 128, 128)
        quantize_weights(2, 1, 1)
        quantize_x(1, 256, 256)
        quantize_x(1, 512, 128)
        quantize_x(1, 640, 128)
        d_neg(1, 0)
        d_neg(1, 1)
        d_pos(1, 0)
        d_neg(1, 2)
        h_mm(1, 0)
        h_mm(1, 1)
        d_pos(1, 1)
        d_pos(1, 2)
        h_mm(1, 2)
        h_mm(1, 3)
        stage_a(0)
        stage_u(0)
        stage_t(0)
        stage_o(0)
        stage_a(1)
        stage_a(2)
        stage_u(1)
        stage_t(1)
        stage_u(2)
        stage_t(2)
        stage_o(1)
        stage_o(2)
